import numpy as np
CORES = [7,63,135,191,263,319,391,447]
N = 8
ROOT = 6
WIDTHS = [128,25,5,128,128,256,256,5]
XW = 256
def setup_inputs(rng):
    return {"x": rng.standard_normal((N, 128, XW), dtype=np.float32)}
def reference(x):
    g = np.concatenate([x[r][:, :WIDTHS[r]] for r in range(N)], axis=1)
    y = np.full((N, 128, g.shape[1]), np.nan, x.dtype)
    y[ROOT] = g
    return {"y": y}

@@ -1,0 +1,90 @@
+from concourse.bass import DstId, RemoteDMATransfer
+
+SCRATCH = {
+    "b0": ("dram", [128, 128], "float32"),
+    "b1": ("dram", [128, 25], "float32"),
+    "b2": ("dram", [128, 5], "float32"),
+    "b3": ("dram", [4, 128, 32], "float32"),
+    "b4": ("dram", [128, 128], "float32"),
+    "b5": ("dram", [2, 128, 128], "float32"),
+    "b7": ("dram", [128, 5], "float32"),
+}
+SEMAPHORES = ["ld", "ld2", "sent", "rl", "a0", "a1", "a2", "a3", "a4", "a5", "a5b", "a7", "st"]
+
+R3_RELAYS = [1, 3, 5, 315]
+R2_RELAY = 0
+ENG = {0: 0xFF, 1: 0xFF, 2: 0x0F, 4: 0xFF, 7: 0x0F}
+CNT = {0: 8, 1: 8, 2: 4, 4: 8, 7: 4}
+
+
+def rank_program(g, core, T, topo):
+    S = T.sem
+    W = T.tables["WIDTHS"]
+    off = [sum(W[:r]) for r in range(len(W))]
+    root = T.cores[6]
+    rank = T.rank_of(core)
+
+    def send(dst, out_ap, in_ap, rsem, mask):
+        rid, pid = topo.addr(dst, core)
+        g.remote_dma(out_ap, in_ap, rsem, S.sent, pid, rid, mask)
+
+    if core == R2_RELAY:
+        g.wait_ge(S.rl, CNT[2])
+        send(root, T.b2[:], T.b2[:], S.a2, ENG[2])
+        g.wait_ge(S.sent, CNT[2])
+        return
+    if core in R3_RELAYS:
+        t = R3_RELAYS.index(core)
+        g.wait_ge(S.rl, 2)
+        send(root, T.b3[t], T.b3[t], S.a3, 0xFF)
+        g.wait_ge(S.sent, 8)
+        return
+    if rank is None:
+        return
+
+    if rank == 6:
+        sy, sc = g.sync, g.scalar
+        n = 0
+        sy.dma_start(T.y[:, off[6]:off[6] + W[6]], T.x[:, 0:W[6]]).then_inc(S.st, 16)
+        sy.wait_ge(S.a4, 8)
+        sy.dma_start(T.y[:, off[4]:off[4] + W[4]], T.b4[:]).then_inc(S.st, 16)
+        sy.wait_ge(S.a5, 8)
+        sy.dma_start(T.y[0:64, off[5]:off[5] + W[5]], T.b5[0]).then_inc(S.st, 16)
+        sy.wait_ge(S.a5b, 8)
+        sy.dma_start(T.y[64:128, off[5]:off[5] + W[5]], T.b5[1]).then_inc(S.st, 16)
+        n += 4
+        for r, cnt in ((7, CNT[7]), (1, CNT[1]), (0, CNT[0]), (2, CNT[2]), (3, 32)):
+            sc.wait_ge(S["a%d" % r], cnt)
+            sc.dma_start(T.y[:, off[r]:off[r] + W[r]], T["b%d" % r][:]).then_inc(S.st, 16)
+            n += 1
+        g.wait_ge(S.st, 16 * n)
+        return
+
+    if rank == 5:
+        g.sync.dma_start(T.b5[0], T.x[0:64, :]).then_inc(S.ld, 16)
+        g.scalar.dma_start(T.b5[1], T.x[64:128, :]).then_inc(S.ld2, 16)
+        g.wait_ge(S.ld, 16)
+        send(root, T.b5[0], T.b5[0], S.a5, 0xFF)
+        g.wait_ge(S.ld2, 16)
+        send(root, T.b5[1], T.b5[1], S.a5b, 0xFF)
+        g.wait_ge(S.sent, 16)
+        return
+    if rank == 3:
+        g.sync.dma_start(T.b3[:], T.x[:, 0:W[3]]).then_inc(S.ld, 16)
+        g.wait_ge(S.ld, 16)
+        trs = []
+        for t, d in enumerate(R3_RELAYS):
+            rid, pid = topo.addr(d, core)
+            trs.append(RemoteDMATransfer(dst_ids=[DstId(rid=rid, pnc=pid)], dma_engine_mask=0x3 << (2 * t),
+                                         remote_sem=S.rl, src=T.b3[t], dst=T.b3[t]))
+        g.remote_dma_fused(trs, local_sem=S.sent)
+        g.wait_ge(S.sent, 8)
+        return
+    buf = T["b%d" % rank]
+    g.sync.dma_start(buf[:], T.x[:, 0:W[rank]]).then_inc(S.ld, 16)
+    g.wait_ge(S.ld, 16)
+    if rank == 2:
+        send(R2_RELAY, buf[:], buf[:], S.rl, ENG[2])
+    else:
+        send(root, buf[:], buf[:], S["a%d" % rank], ENG[rank])
+    g.wait_ge(S.sent, CNT[rank])

@@ -1,7 +1,8 @@
 from concourse.bass import DstId, RemoteDMATransfer
 
 SCRATCH = {
-    "b0": ("dram", [128, 128], "float32"),
+    "b0": ("dram", [128, 96], "float32"),
+    "b0h": ("dram", [128, 32], "float32"),
     "b1": ("dram", [128, 25], "float32"),
     "b2": ("dram", [128, 5], "float32"),
     "b3": ("dram", [4, 128, 32], "float32"),
@@ -9,12 +10,13 @@ SCRATCH = {
     "b5": ("dram", [2, 128, 128], "float32"),
     "b7": ("dram", [128, 5], "float32"),
 }
-SEMAPHORES = ["ld", "ld2", "sent", "rl", "a0", "a1", "a2", "a3", "a4", "a5", "a5b", "a7", "st"]
+SEMAPHORES = ["ld", "ld2", "sent", "rl", "a0", "a0h", "a1", "a2", "a3", "a4", "a5", "a5b", "a7", "st"]
 
-R3_RELAYS = [1, 3, 5, 315]
-R2_RELAY = 0
-ENG = {0: 0xFF, 1: 0xFF, 2: 0x0F, 4: 0xFF, 7: 0x0F}
-CNT = {0: 8, 1: 8, 2: 4, 4: 8, 7: 4}
+R3_RELAYS = [1, 5, 11, 315]
+R0_HELPER = 2
+RELAY = {1: 443, 2: 0}
+ENG = {1: 0xFF, 2: 0x0F, 4: 0xFF, 7: 0x0F}
+CNT = {1: 8, 2: 4, 4: 8, 7: 4}
 
 
 def rank_program(g, core, T, topo):
@@ -28,10 +30,17 @@ def rank_program(g, core, T, topo):
         rid, pid = topo.addr(dst, core)
         g.remote_dma(out_ap, in_ap, rsem, S.sent, pid, rid, mask)
 
-    if core == R2_RELAY:
-        g.wait_ge(S.rl, CNT[2])
-        send(root, T.b2[:], T.b2[:], S.a2, ENG[2])
-        g.wait_ge(S.sent, CNT[2])
+    for r in (1, 2):
+        if core == RELAY[r]:
+            buf = T["b%d" % r]
+            g.wait_ge(S.rl, CNT[r])
+            send(root, buf[:], buf[:], S["a%d" % r], ENG[r])
+            g.wait_ge(S.sent, CNT[r])
+            return
+    if core == R0_HELPER:
+        g.wait_ge(S.rl, 16)
+        send(root, T.b0h[:], T.b0h[:], S.a0h, 0xFF)
+        g.wait_ge(S.sent, 8)
         return
     if core in R3_RELAYS:
         t = R3_RELAYS.index(core)
@@ -44,7 +53,6 @@ def rank_program(g, core, T, topo):
 
     if rank == 6:
         sy, sc = g.sync, g.scalar
-        n = 0
         sy.dma_start(T.y[:, off[6]:off[6] + W[6]], T.x[:, 0:W[6]]).then_inc(S.st, 16)
         sy.wait_ge(S.a4, 8)
         sy.dma_start(T.y[:, off[4]:off[4] + W[4]], T.b4[:]).then_inc(S.st, 16)
@@ -52,14 +60,27 @@ def rank_program(g, core, T, topo):
         sy.dma_start(T.y[0:64, off[5]:off[5] + W[5]], T.b5[0]).then_inc(S.st, 16)
         sy.wait_ge(S.a5b, 8)
         sy.dma_start(T.y[64:128, off[5]:off[5] + W[5]], T.b5[1]).then_inc(S.st, 16)
-        n += 4
-        for r, cnt in ((7, CNT[7]), (1, CNT[1]), (0, CNT[0]), (2, CNT[2]), (3, 32)):
+        sc.wait_ge(S.a7, CNT[7])
+        sc.dma_start(T.y[:, off[7]:off[7] + W[7]], T.b7[:]).then_inc(S.st, 16)
+        sc.wait_ge(S.a0, 8)
+        sc.dma_start(T.y[0:96, 0:W[0]], T.b0[:]).then_inc(S.st, 16)
+        sc.wait_ge(S.a0h, 8)
+        sc.dma_start(T.y[96:128, 0:W[0]], T.b0h[:]).then_inc(S.st, 16)
+        for r, cnt in ((2, CNT[2]), (1, CNT[1]), (3, 32)):
             sc.wait_ge(S["a%d" % r], cnt)
             sc.dma_start(T.y[:, off[r]:off[r] + W[r]], T["b%d" % r][:]).then_inc(S.st, 16)
-            n += 1
-        g.wait_ge(S.st, 16 * n)
+        g.wait_ge(S.st, 16 * 10)
         return
 
+    if rank == 0:
+        g.scalar.dma_start(T.b0h[:], T.x[96:128, 0:W[0]]).then_inc(S.ld2, 16)
+        g.sync.dma_start(T.b0[:], T.x[0:96, 0:W[0]]).then_inc(S.ld, 16)
+        g.wait_ge(S.ld2, 16)
+        send(R0_HELPER, T.b0h[:], T.b0h[:], S.rl, 0xFFFF)
+        g.wait_ge(S.ld, 16)
+        send(root, T.b0[:], T.b0[:], S.a0, 0xFF)
+        g.wait_ge(S.sent, 24)
+        return
     if rank == 5:
         g.sync.dma_start(T.b5[0], T.x[0:64, :]).then_inc(S.ld, 16)
         g.scalar.dma_start(T.b5[1], T.x[64:128, :]).then_inc(S.ld2, 16)
@@ -83,8 +104,8 @@ def rank_program(g, core, T, topo):
     buf = T["b%d" % rank]
     g.sync.dma_start(buf[:], T.x[:, 0:W[rank]]).then_inc(S.ld, 16)
     g.wait_ge(S.ld, 16)
-    if rank == 2:
-        send(R2_RELAY, buf[:], buf[:], S.rl, ENG[2])
+    if rank in RELAY:
+        send(RELAY[rank], buf[:], buf[:], S.rl, ENG[rank])
     else:
         send(root, buf[:], buf[:], S["a%d" % rank], ENG[rank])
     g.wait_ge(S.sent, CNT[rank])

@@ -1,8 +1,9 @@
 from concourse.bass import DstId, RemoteDMATransfer
 
+P0 = 68
 SCRATCH = {
-    "b0": ("dram", [128, 96], "float32"),
-    "b0h": ("dram", [128, 32], "float32"),
+    "b0": ("dram", [128, 68], "float32"),
+    "b0h": ("dram", [3, 128, 20], "float32"),
     "b1": ("dram", [128, 25], "float32"),
     "b2": ("dram", [128, 5], "float32"),
     "b3": ("dram", [4, 128, 32], "float32"),
@@ -13,8 +14,8 @@ SCRATCH = {
 SEMAPHORES = ["ld", "ld2", "sent", "rl", "a0", "a0h", "a1", "a2", "a3", "a4", "a5", "a5b", "a7", "st"]
 
 R3_RELAYS = [1, 5, 11, 315]
-R0_HELPER = 2
-RELAY = {1: 443, 2: 0}
+R0_HELPERS = [0, 2, 4]
+RELAY = {1: 443, 2: 258}
 ENG = {1: 0xFF, 2: 0x0F, 4: 0xFF, 7: 0x0F}
 CNT = {1: 8, 2: 4, 4: 8, 7: 4}
 
@@ -30,6 +31,14 @@ def rank_program(g, core, T, topo):
         rid, pid = topo.addr(dst, core)
         g.remote_dma(out_ap, in_ap, rsem, S.sent, pid, rid, mask)
 
+    def fan(dsts, buf, eng):
+        trs = []
+        for t, d in enumerate(dsts):
+            rid, pid = topo.addr(d, core)
+            trs.append(RemoteDMATransfer(dst_ids=[DstId(rid=rid, pnc=pid)], dma_engine_mask=((1 << eng) - 1) << (eng * t),
+                                         remote_sem=S.rl, src=buf[t], dst=buf[t]))
+        g.remote_dma_fused(trs, local_sem=S.sent)
+
     for r in (1, 2):
         if core == RELAY[r]:
             buf = T["b%d" % r]
@@ -37,9 +46,10 @@ def rank_program(g, core, T, topo):
             send(root, buf[:], buf[:], S["a%d" % r], ENG[r])
             g.wait_ge(S.sent, CNT[r])
             return
-    if core == R0_HELPER:
-        g.wait_ge(S.rl, 16)
-        send(root, T.b0h[:], T.b0h[:], S.a0h, 0xFF)
+    if core in R0_HELPERS:
+        t = R0_HELPERS.index(core)
+        g.wait_ge(S.rl, 4)
+        send(root, T.b0h[t], T.b0h[t], S.a0h, 0xFF)
         g.wait_ge(S.sent, 8)
         return
     if core in R3_RELAYS:
@@ -63,9 +73,9 @@ def rank_program(g, core, T, topo):
         sc.wait_ge(S.a7, CNT[7])
         sc.dma_start(T.y[:, off[7]:off[7] + W[7]], T.b7[:]).then_inc(S.st, 16)
         sc.wait_ge(S.a0, 8)
-        sc.dma_start(T.y[0:96, 0:W[0]], T.b0[:]).then_inc(S.st, 16)
-        sc.wait_ge(S.a0h, 8)
-        sc.dma_start(T.y[96:128, 0:W[0]], T.b0h[:]).then_inc(S.st, 16)
+        sc.dma_start(T.y[0:P0, 0:W[0]], T.b0[:]).then_inc(S.st, 16)
+        sc.wait_ge(S.a0h, 24)
+        sc.dma_start(T.y[P0:128, 0:W[0]], T.b0h[:]).then_inc(S.st, 16)
         for r, cnt in ((2, CNT[2]), (1, CNT[1]), (3, 32)):
             sc.wait_ge(S["a%d" % r], cnt)
             sc.dma_start(T.y[:, off[r]:off[r] + W[r]], T["b%d" % r][:]).then_inc(S.st, 16)
@@ -73,13 +83,13 @@ def rank_program(g, core, T, topo):
         return
 
     if rank == 0:
-        g.scalar.dma_start(T.b0h[:], T.x[96:128, 0:W[0]]).then_inc(S.ld2, 16)
-        g.sync.dma_start(T.b0[:], T.x[0:96, 0:W[0]]).then_inc(S.ld, 16)
+        g.scalar.dma_start(T.b0h[:], T.x[P0:128, 0:W[0]]).then_inc(S.ld2, 16)
+        g.sync.dma_start(T.b0[:], T.x[0:P0, 0:W[0]]).then_inc(S.ld, 16)
         g.wait_ge(S.ld2, 16)
-        send(R0_HELPER, T.b0h[:], T.b0h[:], S.rl, 0xFFFF)
+        fan(R0_HELPERS, T.b0h, 4)
         g.wait_ge(S.ld, 16)
         send(root, T.b0[:], T.b0[:], S.a0, 0xFF)
-        g.wait_ge(S.sent, 24)
+        g.wait_ge(S.sent, 20)
         return
     if rank == 5:
         g.sync.dma_start(T.b5[0], T.x[0:64, :]).then_inc(S.ld, 16)
@@ -93,12 +103,7 @@ def rank_program(g, core, T, topo):
     if rank == 3:
         g.sync.dma_start(T.b3[:], T.x[:, 0:W[3]]).then_inc(S.ld, 16)
         g.wait_ge(S.ld, 16)
-        trs = []
-        for t, d in enumerate(R3_RELAYS):
-            rid, pid = topo.addr(d, core)
-            trs.append(RemoteDMATransfer(dst_ids=[DstId(rid=rid, pnc=pid)], dma_engine_mask=0x3 << (2 * t),
-                                         remote_sem=S.rl, src=T.b3[t], dst=T.b3[t]))
-        g.remote_dma_fused(trs, local_sem=S.sent)
+        fan(R3_RELAYS, T.b3, 2)
         g.wait_ge(S.sent, 8)
         return
     buf = T["b%d" % rank]

from concourse.bass import DstId, RemoteDMATransfer

P0 = 68
SCRATCH = {
    "b0": ("dram", [128, 68], "float32"),
    "b0h": ("dram", [3, 128, 20], "float32"),
    "b1": ("dram", [128, 25], "float32"),
    "b2": ("dram", [128, 5], "float32"),
    "b3": ("dram", [4, 128, 32], "float32"),
    "b4": ("dram", [128, 128], "float32"),
    "b5": ("dram", [2, 128, 128], "float32"),
    "b7": ("dram", [128, 5], "float32"),
}
SEMAPHORES = ["ld", "ld2", "sent", "rl", "a0", "a0h", "a1", "a2", "a3", "a4", "a5", "a5b", "a7", "st"]

R3_RELAYS = [1, 5, 11, 315]
R0_HELPERS = [0, 2, 4]
RELAY = {1: 443, 2: 258}
ENG = {1: 0xFF, 2: 0x0F, 4: 0xFF, 7: 0x0F}
CNT = {1: 8, 2: 4, 4: 8, 7: 4}


def rank_program(g, core, T, topo):
    S = T.sem
    W = T.tables["WIDTHS"]
    off = [sum(W[:r]) for r in range(len(W))]
    root = T.cores[6]
    rank = T.rank_of(core)

    def send(dst, out_ap, in_ap, rsem, mask):
        rid, pid = topo.addr(dst, core)
        g.remote_dma(out_ap, in_ap, rsem, S.sent, pid, rid, mask)

    def fan(dsts, buf, eng):
        trs = []
        for t, d in enumerate(dsts):
            rid, pid = topo.addr(d, core)
            trs.append(RemoteDMATransfer(dst_ids=[DstId(rid=rid, pnc=pid)], dma_engine_mask=((1 << eng) - 1) << (eng * t),
                                         remote_sem=S.rl, src=buf[t], dst=buf[t]))
        g.remote_dma_fused(trs, local_sem=S.sent)

    for r in (1, 2):
        if core == RELAY[r]:
            buf = T["b%d" % r]
            g.wait_ge(S.rl, CNT[r])
            send(root, buf[:], buf[:], S["a%d" % r], ENG[r])
            g.wait_ge(S.sent, CNT[r])
            return
    if core in R0_HELPERS:
        t = R0_HELPERS.index(core)
        g.wait_ge(S.rl, 4)
        send(root, T.b0h[t], T.b0h[t], S.a0h, 0xFF)
        g.wait_ge(S.sent, 8)
        return
    if core in R3_RELAYS:
        t = R3_RELAYS.index(core)
        g.wait_ge(S.rl, 2)
        send(root, T.b3[t], T.b3[t], S.a3, 0xFF)
        g.wait_ge(S.sent, 8)
        return
    if rank is None:
        return

    if rank == 6:
        sy, sc = g.sync, g.scalar
        sy.dma_start(T.y[:, off[6]:off[6] + W[6]], T.x[:, 0:W[6]]).then_inc(S.st, 16)
        sy.wait_ge(S.a4, 8)
        sy.dma_start(T.y[:, off[4]:off[4] + W[4]], T.b4[:]).then_inc(S.st, 16)
        sy.wait_ge(S.a5, 8)
        sy.dma_start(T.y[0:64, off[5]:off[5] + W[5]], T.b5[0]).then_inc(S.st, 16)
        sy.wait_ge(S.a5b, 8)
        sy.dma_start(T.y[64:128, off[5]:off[5] + W[5]], T.b5[1]).then_inc(S.st, 16)
        sc.wait_ge(S.a7, CNT[7])
        sc.dma_start(T.y[:, off[7]:off[7] + W[7]], T.b7[:]).then_inc(S.st, 16)
        sc.wait_ge(S.a0, 8)
        sc.dma_start(T.y[0:P0, 0:W[0]], T.b0[:]).then_inc(S.st, 16)
        sc.wait_ge(S.a0h, 24)
        sc.dma_start(T.y[P0:128, 0:W[0]], T.b0h[:]).then_inc(S.st, 16)
        for r, cnt in ((2, CNT[2]), (1, CNT[1]), (3, 32)):
            sc.wait_ge(S["a%d" % r], cnt)
            sc.dma_start(T.y[:, off[r]:off[r] + W[r]], T["b%d" % r][:]).then_inc(S.st, 16)
        g.wait_ge(S.st, 16 * 10)
        return

    if rank == 0:
        g.scalar.dma_start(T.b0h[:], T.x[P0:128, 0:W[0]]).then_inc(S.ld2, 16)
        g.sync.dma_start(T.b0[:], T.x[0:P0, 0:W[0]]).then_inc(S.ld, 16)
        g.wait_ge(S.ld2, 16)
        fan(R0_HELPERS, T.b0h, 4)
        g.wait_ge(S.ld, 16)
        send(root, T.b0[:], T.b0[:], S.a0, 0xFF)
        g.wait_ge(S.sent, 20)
        return
    if rank == 5:
        g.sync.dma_start(T.b5[0], T.x[0:64, :]).then_inc(S.ld, 16)
        g.scalar.dma_start(T.b5[1], T.x[64:128, :]).then_inc(S.ld2, 16)
        g.wait_ge(S.ld, 16)
        send(root, T.b5[0], T.b5[0], S.a5, 0xFF)
        g.wait_ge(S.ld2, 16)
        send(root, T.b5[1], T.b5[1], S.a5b, 0xFF)
        g.wait_ge(S.sent, 16)
        return
    if rank == 3:
        g.sync.dma_start(T.b3[:], T.x[:, 0:W[3]]).then_inc(S.ld, 16)
        g.wait_ge(S.ld, 16)
        fan(R3_RELAYS, T.b3, 2)
        g.wait_ge(S.sent, 8)
        return
    buf = T["b%d" % rank]
    g.sync.dma_start(buf[:], T.x[:, 0:W[rank]]).then_inc(S.ld, 16)
    g.wait_ge(S.ld, 16)
    if rank in RELAY:
        send(RELAY[rank], buf[:], buf[:], S.rl, ENG[rank])
    else:
        send(root, buf[:], buf[:], S["a%d" % rank], ENG[rank])
    g.wait_ge(S.sent, CNT[rank])
